import numpy as np
import ml_dtypes


def mxq(x, axis, fmt="e4m3"):
    dtype, down = {"e4m3": (ml_dtypes.float8_e4m3fn, 7), "e5m2": (ml_dtypes.float8_e5m2, 14)}[fmt]
    v = np.moveaxis(np.asarray(x, np.float32).astype(ml_dtypes.bfloat16).astype(np.float64), axis, -1)
    blocks = v.reshape(v.shape[:-1] + (-1, 32))
    amax = np.abs(blocks).max(-1, keepdims=True)
    byte = np.maximum(np.where(amax > 0, np.frexp(amax)[1] - 1 + 127, 0) - down, 1)
    scale = np.exp2(byte - 127.0)
    codes = (blocks / scale).astype(np.float32).astype(dtype).astype(np.float64)
    return np.moveaxis((codes * scale).reshape(v.shape), -1, axis)


WIDE = False


def mx_kscale(k):
    if not WIDE:
        return np.ones(k)
    levels = np.array([10, -10, 5, -5, 0])
    if k % 512:
        return np.exp2(np.random.permutation(np.resize(levels, k // 32))).repeat(32)
    a = np.empty((k // 512, 16))
    for p in range(k // 512):
        a[p, :8] = np.random.permutation(np.resize(levels, 8))
        for g in range(8):
            far = levels[np.abs(levels - a[p, g]) >= 10]
            a[p, g + 8] = far[np.random.randint(len(far))]
    return np.exp2(a.ravel()).repeat(32)


def f64(x):
    return np.asarray(x).astype(np.float64)


def striped(idx):
    return np.tile(idx.reshape(-1, 16).T, (8, 1)).astype(np.uint16)


def unstriped(offs):
    return offs[:16].T.reshape(-1).astype(np.int64)


def striped8(idx):
    return np.concatenate([x.reshape(-1, 16).T for x in idx]).astype(np.uint16)


def runs(offs, k):
    lists = np.stack([offs[16 * r : 16 * r + 16].T.reshape(-1) for r in range(8)]).astype(np.int64)
    return lists[np.arange(k) % 512 // 64]


def pack_weight(w):
    k, n = w.shape
    w = f64(np.asarray(w, np.float32).astype(ml_dtypes.bfloat16)).reshape(k // 32, 32, n)
    amax = np.abs(w).max(1)
    byte = np.clip(np.where(amax > 0, np.frexp(amax)[1] - 1 + 127 - 7, 1), 1, 254)
    scaled = (w * np.exp2(127.0 - byte)[:, None, :]).reshape(k, n).astype(np.float32)
    words = np.ascontiguousarray(scaled.reshape(k // 512, 128, 4, n).transpose(0, 1, 3, 2)).astype(ml_dtypes.float8_e4m3fn).view(np.uint8)
    return words, np.ascontiguousarray(byte.astype(np.uint8).reshape(k // 512, 16, n))


def unpack_weight(words, scales):
    g, p, n, _ = words.shape
    vals = np.ascontiguousarray(words).view(ml_dtypes.float8_e4m3fn).astype(np.float64) * np.repeat(np.exp2(scales.astype(np.float64) - 127.0), 8, axis=1)[..., None]
    return vals.transpose(0, 1, 3, 2).reshape(g * 512, n)


K, T, S, V, H = 512, 2048, 512, 512, 512


def setup_inputs():
    n = np.random.standard_normal
    s = mx_kscale(K)[:, None]
    u = mx_kscale(S)
    packed_xT = pack_weight(n((K, T)) * s)
    return {
        "x_words": packed_xT[0],
        "x_scales": packed_xT[1],
        "w1": (n((K, H)) / np.sqrt(K) / s).astype(np.float32),
        "w2": (n((K, H)) / np.sqrt(K) / s).astype(np.float32),
        "w3": (n((K, H)) / np.sqrt(K) / s).astype(np.float32),
        "ga": (np.random.uniform(0.5, 1.5, (H, 1)) * u[:, None]).astype(np.float32),
        "gb": (np.random.uniform(0.5, 1.5, (H, 1)) / u[:, None]).astype(np.float32),
        "offs": striped(np.random.permutation(T)[:S]),
        "two": striped(np.random.permutation(T)[:S]),
        "n1": striped8(np.stack([np.random.permutation(S) for _ in range(8)])),
        "n2": striped8(np.stack([np.random.permutation(S) for _ in range(8)])),
        "three": striped(np.random.permutation(T)[:V]),
        "n3": striped8(np.stack([np.random.permutation(V) for _ in range(8)])),
        "n4": striped8(np.stack([np.random.permutation(V) for _ in range(8)])),
        "n5": striped8(np.stack([np.random.permutation(V) for _ in range(8)])),
        "n6": striped8(np.stack([np.random.permutation(V) for _ in range(8)])),
        "n7": striped8(np.stack([np.random.permutation(V) for _ in range(8)])),
    }


def reference(x_words, x_scales, w1, w2, w3, ga, gb, offs, two, n1, n2, three, n3, n4, n5, n6, n7):
    xq = unpack_weight(x_words, x_scales)[:, unstriped(offs)]
    y = mxq(f64(w1), 0, "e4m3").T @ xq
    x_two = unpack_weight(x_words, x_scales)[:, unstriped(two)]
    d = mxq(f64(w2), 0, "e4m3").T @ x_two
    z = f64(ga) * (y[np.arange(H)[:, None], runs(n1, H)] - (np.tanh(d) * (d[np.arange(H)[:, None], runs(n2, H)])))
    x_three = unpack_weight(x_words, x_scales)[:, unstriped(three)]
    b = mxq(f64(w3), 0, "e4m3").T @ x_three
    sq = (b) ** 2
    z2 = f64(gb) * ((b[np.arange(H)[:, None], runs(n4, H)]) / (np.sqrt(sq + sq[np.arange(H)[:, None], runs(n3, H)] + 0.25)))
    s = 0.0625 * ((mxq(z, 0, "e4m3").T @ mxq(z2, 0, "e4m3")))
    b1 = s[np.arange(S)[:, None], runs(n5, S)]
    b2 = s[np.arange(S)[:, None], runs(n6, S)]
    b3 = s[np.arange(S)[:, None], runs(n7, S)]
    return np.maximum(np.maximum(b1, b2), b3) - (0.5 * (np.maximum(np.minimum(b1, b2), np.minimum(np.maximum(b1, b2), b3))))

@@ -1,0 +1,188 @@
+from contextlib import ExitStack
+
+import concourse.mybir as mybir
+
+F32 = mybir.dt.float32
+BF16 = mybir.dt.bfloat16
+I32 = mybir.dt.int32
+U32 = mybir.dt.uint32
+U16 = mybir.dt.uint16
+U8 = mybir.dt.uint8
+FP8X4 = mybir.dt.float8_e4m3fn_x4
+ALU = mybir.AluOpType
+ACT = mybir.ActivationFunctionType
+
+P = 128
+PACK = 4
+N = 512
+T = 2048
+WIN = 2 * N
+
+FLOPS = 4 * 2 * 512 * 512 * 512
+
+
+def tile_picked_twksoftbrmstop2_none_p_kernel(
+    tc, x_words, x_scales, w1, w2, w3, ga, gb, offs, two, n1, n2, three, n3, n4, n5, n6, n7, out
+):
+    nc = tc.nc
+    with ExitStack() as ctx:
+        keep = ctx.enter_context(tc.tile_pool(name="keep", bufs=1))
+        ring = ctx.enter_context(tc.tile_pool(name="ring", bufs=2))
+        psum = ctx.enter_context(tc.psum_pool(name="psum", bufs=8))
+
+        def load_list(name, src):
+            tile = keep.tile([P, N // 16], U16, name="list_" + name)
+            nc.sync.dma_start(tile[:], src)
+            return tile
+
+        def load_weight(name, w):
+            halves = []
+            for h in range(2):
+                raw = keep.tile([P, PACK, N // 2], F32, name="raw_%s_%d" % (name, h))
+                nc.sync.dma_start(raw[:], w.rearrange("(p j) c -> p j c", j=PACK)[:, :, h * (N // 2) : (h + 1) * (N // 2)])
+                halves.append(raw)
+            return halves
+
+        xs = keep.tile([P, T], U8, name="xs", align_bytes=64)
+        nc.vector.memset(xs[:].bitcast(I32), 0)
+        for q in range(4):
+            nc.scalar.dma_start(xs[32 * q : 32 * q + 4, :].bitcast(I32), x_scales[0, 4 * q : 4 * q + 4, :].bitcast(I32))
+
+        lists = {}
+        lists["two"] = load_list("two", two)
+        raw2 = load_weight("w2", w2)
+        lists["three"] = load_list("three", three)
+        xw = keep.tile([P, T], U32, name="xw", align_bytes=64)
+        nc.sync.dma_start(xw[:].bitcast(I32), x_words[0].rearrange("p c r -> p (c r)").bitcast(I32))
+        lists["offs"] = load_list("offs", offs)
+        ga_t = keep.tile([P, PACK], F32, name="ga_t")
+        gb_t = keep.tile([P, PACK], F32, name="gb_t")
+        nc.scalar.dma_start(ga_t[:], ga.rearrange("(p t) o -> p (t o)", t=PACK))
+        nc.scalar.dma_start(gb_t[:], gb.rearrange("(p t) o -> p (t o)", t=PACK))
+        raw3 = load_weight("w3", w3)
+        lists["n2"] = load_list("n2", n2)
+        raw1 = load_weight("w1", w1)
+        for name, src in (("n3", n3), ("n4", n4), ("n1", n1), ("n5", n5), ("n6", n6), ("n7", n7)):
+            lists[name] = load_list(name, src)
+
+        win_a = [keep.tile([P, WIN], F32, name="win_a%d" % t) for t in range(PACK)]
+        win_b = [keep.tile([P, WIN], F32, name="win_b%d" % t) for t in range(PACK)]
+        for win in win_a + win_b:
+            nc.vector.memset(win[:, N:], 0.0)
+
+        def gather_scales(name):
+            tile = keep.tile([P, N], U8, name="picked_scales_" + name, align_bytes=64)
+            nc.vector.tensor_copy(tile[:], xs[:].indirect(lists[name][:]))
+            return tile
+
+        def gather_words(name):
+            tile = keep.tile([P, N], U32, name="picked_words_" + name, align_bytes=64)
+            nc.vector.tensor_copy(tile[:], xw[:].indirect(lists[name][:]))
+            return tile
+
+        def weave_weight(name, halves):
+            woven = keep.tile([P, PACK * N], BF16, name="woven_" + name, align_bytes=64)
+            dst = woven[:].rearrange("p (t m j) -> p m j t", t=PACK, j=PACK)
+            for h, raw in enumerate(halves):
+                nc.scalar.copy(dst[:, h * (P // 2) : (h + 1) * (P // 2)], raw[:].rearrange("p j (m t) -> p m j t", t=PACK))
+            return woven
+
+        def quantize(name, woven, width):
+            codes = keep.tile([P, width], U32, name="codes_" + name, align_bytes=64)
+            scales = keep.tile([P, width], U8, name="scales_" + name, align_bytes=64)
+            nc.vector.quantize_mx(out=codes[:].bitcast(FP8X4), scales=scales[:], in_=woven[:])
+            return codes, scales
+
+        def product(stationary, t, moving):
+            acc = psum.tile([P, N], F32, name="acc")
+            cols = slice(t * P, (t + 1) * P)
+            nc.tensor.matmul_mx(
+                out=acc[:],
+                lhsT=stationary[0][:, cols].bitcast(FP8X4),
+                lhsT_scale=stationary[1][:, cols],
+                rhs=moving[0][:].bitcast(FP8X4),
+                rhs_scale=moving[1][:],
+                start=True,
+                stop=True,
+            )
+            return acc
+
+        def fused(dst, win, name, other, op):
+            nc.vector.tensor_tensor(dst, win[:].indirect(lists[name][:]), other, op)
+
+        sc = {name: gather_scales(name) for name in ("two", "three", "offs")}
+        woven2 = weave_weight("w2", raw2)
+        x_two = (gather_words("two"), sc["two"])
+        q2 = quantize("w2", woven2, N)
+        x_three = (gather_words("three"), sc["three"])
+        x_offs = (gather_words("offs"), sc["offs"])
+
+        tanh_d = keep.tile([P, PACK, N], F32, name="tanh_d")
+        prod = keep.tile([P, PACK, N], F32, name="prod")
+        for t in range(PACK):
+            acc = product(q2, t, x_two)
+            nc.scalar.activation(win_a[t][:, :N], acc[:], ACT.Copy, scale=ga_t[:, t : t + 1])
+            nc.scalar.activation(tanh_d[:, t, :], acc[:], ACT.Tanh)
+        woven3 = weave_weight("w3", raw3)
+        for t in range(PACK):
+            fused(prod[:, t, :], win_a[t], "n2", tanh_d[:, t, :], ALU.mult)
+        q3 = quantize("w3", woven3, N)
+
+        sq = keep.tile([P, PACK, N], F32, name="sq")
+        den = keep.tile([P, PACK, N], F32, name="den")
+        rs = keep.tile([P, PACK, N], F32, name="rs")
+        z2 = keep.tile([P, PACK, N], F32, name="z2")
+        z = keep.tile([P, PACK, N], F32, name="z")
+        for t in range(PACK):
+            acc = product(q3, t, x_three)
+            nc.scalar.activation(win_b[t][:, :N], acc[:], ACT.Square)
+            nc.scalar.activation(sq[:, t, :], acc[:], ACT.Square)
+            nc.scalar.activation(win_a[t][:, :N], acc[:], ACT.Copy, scale=gb_t[:, t : t + 1])
+        woven1 = weave_weight("w1", raw1)
+        for t in range(PACK):
+            fused(den[:, t, :], win_b[t], "n3", sq[:, t, :], ALU.add)
+            nc.scalar.activation(rs[:, t, :], den[:, t, :], ACT.Abs_reciprocal_sqrt, bias=0.25)
+        q1 = quantize("w1", woven1, N)
+        for t in range(PACK):
+            fused(z2[:, t, :], win_a[t], "n4", rs[:, t, :], ALU.mult)
+        for t in range(PACK):
+            acc = product(q1, t, x_offs)
+            nc.scalar.activation(win_b[t][:, :N], acc[:], ACT.Copy, scale=ga_t[:, t : t + 1])
+        woven_z2 = keep.tile([P, PACK * N], BF16, name="woven_z2", align_bytes=64)
+        nc.scalar.copy(
+            woven_z2[:].rearrange("p (c i t) -> p c t i", i=4, t=PACK),
+            z2[:].rearrange("p t (c i) -> p c t i", i=4),
+        )
+        for t in range(PACK):
+            fused(z[:, t, :], win_b[t], "n1", prod[:, t, :], ALU.subtract)
+        qz2 = quantize("z2", woven_z2, N)
+
+        first = keep.tile([P, N], BF16, name="woven_z_first", align_bytes=64)
+        rest = keep.tile([P, (PACK - 1) * N], BF16, name="woven_z_rest", align_bytes=64)
+        z_view = z[:].rearrange("p t (m u) -> p m t u", u=PACK)
+        nc.vector.tensor_copy(first[:].rearrange("p (m t) -> p m t", t=PACK), z_view[:, :, :, 0])
+        nc.scalar.copy(rest[:].rearrange("p (u m t) -> p m t u", u=PACK - 1, t=PACK), z_view[:, :, :, 1:])
+        out_rows = out.rearrange("(p u) v -> u p v", u=PACK)
+        for u in range(PACK):
+            src = first[:] if u == 0 else rest[:, (u - 1) * N : u * N]
+            qz = quantize("zu%d" % u, src, P)
+            acc = product(qz, 0, qz2)
+            win = win_a[u]
+            nc.scalar.activation(win[:, :N], acc[:], ACT.Copy, scale=0.03125)
+            a = ring.tile([P, N], F32, name="a")
+            d = ring.tile([P, N], F32, name="d")
+            half_max = ring.tile([P, N], F32, name="half_max")
+            gap = ring.tile([P, N], F32, name="gap")
+            e = ring.tile([P, N], F32, name="e")
+            low = ring.tile([P, N], F32, name="low")
+            lift = ring.tile([P, N], F32, name="lift")
+            res = ring.tile([P, N], F32, name="res")
+            nc.vector.tensor_copy(a[:], win[:].indirect(lists["n5"][:]))
+            fused(d[:], win, "n6", a[:], ALU.subtract)
+            nc.vector.scalar_tensor_tensor(half_max[:], d[:], 0.0, a[:], ALU.max, ALU.add)
+            nc.scalar.activation(gap[:], d[:], ACT.Abs)
+            fused(e[:], win, "n7", half_max[:], ALU.subtract)
+            nc.vector.scalar_tensor_tensor(low[:], e[:], -1.0, gap[:], ALU.mult, ALU.min)
+            nc.vector.scalar_tensor_tensor(lift[:], e[:], 2.0, low[:], ALU.mult, ALU.max)
+            nc.vector.tensor_tensor(res[:], lift[:], half_max[:], ALU.add)
+            nc.sync.dma_start(out_rows[u], res[:])

@@ -1,6 +1,7 @@
 from contextlib import ExitStack
 
 import concourse.mybir as mybir
+from concourse.masks import make_identity
 
 F32 = mybir.dt.float32
 BF16 = mybir.dt.bfloat16
@@ -27,8 +28,8 @@ def tile_picked_twksoftbrmstop2_none_p_kernel(
     nc = tc.nc
     with ExitStack() as ctx:
         keep = ctx.enter_context(tc.tile_pool(name="keep", bufs=1))
-        ring = ctx.enter_context(tc.tile_pool(name="ring", bufs=2))
-        psum = ctx.enter_context(tc.psum_pool(name="psum", bufs=8))
+        ring = ctx.enter_context(tc.tile_pool(name="ring", bufs=4))
+        psum = ctx.enter_context(tc.psum_pool(name="psum", bufs=1))
 
         def load_list(name, src):
             tile = keep.tile([P, N // 16], U16, name="list_" + name)
@@ -50,23 +51,23 @@ def tile_picked_twksoftbrmstop2_none_p_kernel(
 
         lists = {}
         lists["two"] = load_list("two", two)
-        raw2 = load_weight("w2", w2)
         lists["three"] = load_list("three", three)
+        lists["offs"] = load_list("offs", offs)
         xw = keep.tile([P, T], U32, name="xw", align_bytes=64)
         nc.sync.dma_start(xw[:].bitcast(I32), x_words[0].rearrange("p c r -> p (c r)").bitcast(I32))
-        lists["offs"] = load_list("offs", offs)
+        raw2 = load_weight("w2", w2)
+        raw3 = load_weight("w3", w3)
         ga_t = keep.tile([P, PACK], F32, name="ga_t")
         gb_t = keep.tile([P, PACK], F32, name="gb_t")
-        nc.scalar.dma_start(ga_t[:], ga.rearrange("(p t) o -> p (t o)", t=PACK))
-        nc.scalar.dma_start(gb_t[:], gb.rearrange("(p t) o -> p (t o)", t=PACK))
-        raw3 = load_weight("w3", w3)
+        nc.sync.dma_start(ga_t[:], ga.rearrange("(p t) o -> p (t o)", t=PACK))
         lists["n2"] = load_list("n2", n2)
         raw1 = load_weight("w1", w1)
+        nc.sync.dma_start(gb_t[:], gb.rearrange("(p t) o -> p (t o)", t=PACK))
         for name, src in (("n3", n3), ("n4", n4), ("n1", n1), ("n5", n5), ("n6", n6), ("n7", n7)):
             lists[name] = load_list(name, src)
 
         win_a = [keep.tile([P, WIN], F32, name="win_a%d" % t) for t in range(PACK)]
-        win_b = [keep.tile([P, WIN], F32, name="win_b%d" % t) for t in range(PACK)]
+        win_b = [keep.tile([P, WIN], F32, name="win_b%d" % t, align_bytes=64) for t in range(PACK)]
         for win in win_a + win_b:
             nc.vector.memset(win[:, N:], 0.0)
 
@@ -75,16 +76,16 @@ def tile_picked_twksoftbrmstop2_none_p_kernel(
             nc.vector.tensor_copy(tile[:], xs[:].indirect(lists[name][:]))
             return tile
 
-        def gather_words(name):
-            tile = keep.tile([P, N], U32, name="picked_words_" + name, align_bytes=64)
+        def gather_words(name, tag=None):
+            tile = keep.tile([P, N], U32, name="picked_words_" + name, tag=tag or "picked_words_" + name, align_bytes=64)
             nc.vector.tensor_copy(tile[:], xw[:].indirect(lists[name][:]))
             return tile
 
-        def weave_weight(name, halves):
+        def weave_weight(name, halves, copies):
             woven = keep.tile([P, PACK * N], BF16, name="woven_" + name, align_bytes=64)
             dst = woven[:].rearrange("p (t m j) -> p m j t", t=PACK, j=PACK)
             for h, raw in enumerate(halves):
-                nc.scalar.copy(dst[:, h * (P // 2) : (h + 1) * (P // 2)], raw[:].rearrange("p j (m t) -> p m j t", t=PACK))
+                copies[h](dst[:, h * (P // 2) : (h + 1) * (P // 2)], raw[:].rearrange("p j (m t) -> p m j t", t=PACK))
             return woven
 
         def quantize(name, woven, width):
@@ -93,8 +94,8 @@ def tile_picked_twksoftbrmstop2_none_p_kernel(
             nc.vector.quantize_mx(out=codes[:].bitcast(FP8X4), scales=scales[:], in_=woven[:])
             return codes, scales
 
-        def product(stationary, t, moving):
-            acc = psum.tile([P, N], F32, name="acc")
+        def product(stationary, t, moving, bank):
+            acc = psum.tile([P, N], F32, name="bank%d" % bank)
             cols = slice(t * P, (t + 1) * P)
             nc.tensor.matmul_mx(
                 out=acc[:],
@@ -110,79 +111,139 @@ def tile_picked_twksoftbrmstop2_none_p_kernel(
         def fused(dst, win, name, other, op):
             nc.vector.tensor_tensor(dst, win[:].indirect(lists[name][:]), other, op)
 
-        sc = {name: gather_scales(name) for name in ("two", "three", "offs")}
-        woven2 = weave_weight("w2", raw2)
-        x_two = (gather_words("two"), sc["two"])
+        ident = keep.tile([P, P], F32, name="ident")
+        make_identity(nc, ident[:])
+
+        picked_scales = {name: gather_scales(name) for name in ("two", "three", "offs")}
+        woven2 = weave_weight("w2", raw2, (nc.scalar.copy, nc.scalar.copy))
+        woven3 = weave_weight("w3", raw3, (nc.scalar.copy, nc.scalar.copy))
         q2 = quantize("w2", woven2, N)
-        x_three = (gather_words("three"), sc["three"])
-        x_offs = (gather_words("offs"), sc["offs"])
+        q3 = quantize("w3", woven3, N)
+        x_two = (gather_words("two"), picked_scales["two"])
+        x_three = (gather_words("three"), picked_scales["three"])
+        x_offs = (gather_words("offs", "woven_w2"), picked_scales["offs"])
 
         tanh_d = keep.tile([P, PACK, N], F32, name="tanh_d")
         prod = keep.tile([P, PACK, N], F32, name="prod")
-        for t in range(PACK):
-            acc = product(q2, t, x_two)
-            nc.scalar.activation(win_a[t][:, :N], acc[:], ACT.Copy, scale=ga_t[:, t : t + 1])
-            nc.scalar.activation(tanh_d[:, t, :], acc[:], ACT.Tanh)
-        woven3 = weave_weight("w3", raw3)
-        for t in range(PACK):
-            fused(prod[:, t, :], win_a[t], "n2", tanh_d[:, t, :], ALU.mult)
-        q3 = quantize("w3", woven3, N)
-
         sq = keep.tile([P, PACK, N], F32, name="sq")
         den = keep.tile([P, PACK, N], F32, name="den")
         rs = keep.tile([P, PACK, N], F32, name="rs")
         z2 = keep.tile([P, PACK, N], F32, name="z2")
-        z = keep.tile([P, PACK, N], F32, name="z")
+        z = keep.tile([P, PACK * N], F32, name="z", align_bytes=64)
+        acc_b = []
+
+        def square(t):
+            acc_b.append(product(q3, t, x_three, PACK + t))
+            nc.scalar.activation(win_b[t][:, :N], acc_b[t][:], ACT.Square)
+            nc.sync.dma_start(sq[:, t, :], win_b[t][:, :N])
+
         for t in range(PACK):
-            acc = product(q3, t, x_three)
-            nc.scalar.activation(win_b[t][:, :N], acc[:], ACT.Square)
-            nc.scalar.activation(sq[:, t, :], acc[:], ACT.Square)
-            nc.scalar.activation(win_a[t][:, :N], acc[:], ACT.Copy, scale=gb_t[:, t : t + 1])
-        woven1 = weave_weight("w1", raw1)
+            acc = product(q2, t, x_two, t)
+            nc.scalar.activation(win_a[t][:, :N], acc[:], ACT.Copy, scale=ga_t[:, t : t + 1])
+            nc.scalar.activation(tanh_d[:, t, :], acc[:], ACT.Tanh)
+            fused(prod[:, t, :], win_a[t], "n2", tanh_d[:, t, :], ALU.mult)
+            if t > 0:
+                square(t - 1)
+        square(PACK - 1)
+        woven1 = weave_weight("w1", raw1, (nc.scalar.copy, nc.scalar.copy))
+        q1 = quantize("w1", woven1, N)
         for t in range(PACK):
+            nc.scalar.activation(win_a[t][:, :N], acc_b[t][:], ACT.Copy, scale=gb_t[:, t : t + 1])
             fused(den[:, t, :], win_b[t], "n3", sq[:, t, :], ALU.add)
             nc.scalar.activation(rs[:, t, :], den[:, t, :], ACT.Abs_reciprocal_sqrt, bias=0.25)
-        q1 = quantize("w1", woven1, N)
         for t in range(PACK):
             fused(z2[:, t, :], win_a[t], "n4", rs[:, t, :], ALU.mult)
         for t in range(PACK):
-            acc = product(q1, t, x_offs)
+            acc = product(q1, t, x_offs, t)
             nc.scalar.activation(win_b[t][:, :N], acc[:], ACT.Copy, scale=ga_t[:, t : t + 1])
-        woven_z2 = keep.tile([P, PACK * N], BF16, name="woven_z2", align_bytes=64)
-        nc.scalar.copy(
-            woven_z2[:].rearrange("p (c i t) -> p c t i", i=4, t=PACK),
-            z2[:].rearrange("p t (c i) -> p c t i", i=4),
-        )
+        codes_z2 = keep.tile([P, N], U32, name="codes_z2", align_bytes=64)
+        scales_z2 = keep.tile([P, N], U8, name="scales_z2", align_bytes=64)
+        for h in range(2):
+            cols = slice(h * (N // 2), (h + 1) * (N // 2))
+            woven = z[:, (1 + h) * N : (2 + h) * N].bitcast(BF16)
+            nc.scalar.copy(
+                woven.rearrange("p (c i t) -> p c t i", i=4, t=PACK),
+                z2[:, :, cols].rearrange("p t (c i) -> p c t i", i=4),
+            )
+            nc.vector.quantize_mx(out=codes_z2[:, cols].bitcast(FP8X4), scales=scales_z2[:, cols], in_=woven)
+        qz2 = (codes_z2, scales_z2)
         for t in range(PACK):
-            fused(z[:, t, :], win_b[t], "n1", prod[:, t, :], ALU.subtract)
-        qz2 = quantize("z2", woven_z2, N)
+            fused(z[:, t * N : (t + 1) * N], win_b[t], "n1", prod[:, t, :], ALU.subtract)
 
         first = keep.tile([P, N], BF16, name="woven_z_first", align_bytes=64)
         rest = keep.tile([P, (PACK - 1) * N], BF16, name="woven_z_rest", align_bytes=64)
-        z_view = z[:].rearrange("p t (m u) -> p m t u", u=PACK)
+        z_view = z[:].rearrange("p (t m u) -> p m t u", t=PACK, u=PACK)
         nc.vector.tensor_copy(first[:].rearrange("p (m t) -> p m t", t=PACK), z_view[:, :, :, 0])
         nc.scalar.copy(rest[:].rearrange("p (u m t) -> p m t u", u=PACK - 1, t=PACK), z_view[:, :, :, 1:])
         out_rows = out.rearrange("(p u) v -> u p v", u=PACK)
-        for u in range(PACK):
+
+        def plane(name):
+            return ring.tile([P, N], F32, name=name)
+
+        def scores(u, scale):
             src = first[:] if u == 0 else rest[:, (u - 1) * N : u * N]
             qz = quantize("zu%d" % u, src, P)
-            acc = product(qz, 0, qz2)
-            win = win_a[u]
-            nc.scalar.activation(win[:, :N], acc[:], ACT.Copy, scale=0.03125)
-            a = ring.tile([P, N], F32, name="a")
-            d = ring.tile([P, N], F32, name="d")
-            half_max = ring.tile([P, N], F32, name="half_max")
-            gap = ring.tile([P, N], F32, name="gap")
-            e = ring.tile([P, N], F32, name="e")
-            low = ring.tile([P, N], F32, name="low")
-            lift = ring.tile([P, N], F32, name="lift")
-            res = ring.tile([P, N], F32, name="res")
-            nc.vector.tensor_copy(a[:], win[:].indirect(lists["n5"][:]))
-            fused(d[:], win, "n6", a[:], ALU.subtract)
-            nc.vector.scalar_tensor_tensor(half_max[:], d[:], 0.0, a[:], ALU.max, ALU.add)
-            nc.scalar.activation(gap[:], d[:], ACT.Abs)
-            fused(e[:], win, "n7", half_max[:], ALU.subtract)
-            nc.vector.scalar_tensor_tensor(low[:], e[:], -1.0, gap[:], ALU.mult, ALU.min)
-            nc.vector.scalar_tensor_tensor(lift[:], e[:], 2.0, low[:], ALU.mult, ALU.max)
-            nc.vector.tensor_tensor(res[:], lift[:], half_max[:], ALU.add)
-            nc.sync.dma_start(out_rows[u], res[:])
+            acc = product(qz, 0, qz2, PACK + u)
+            if u == 0:
+                nc.vector.tensor_scalar(win_a[u][:, :N], acc[:], scale, None, ALU.mult)
+            else:
+                nc.scalar.activation(win_a[u][:, :N], acc[:], ACT.Copy, scale=scale)
+
+        def turned_sum(terms, width, bank):
+            acc = psum.tile([P, N], F32, name="bank%d" % bank)
+            steps = [(term, slice(b * P, (b + 1) * P)) for term in terms for b in range(width // P)]
+            for k, (term, cols) in enumerate(steps):
+                nc.tensor.matmul(acc[:, cols], term[:, cols], ident[:], start=k == 0, stop=k == len(steps) - 1, is_transpose=True)
+            return acc[:, :width]
+
+        def looked_up(u, name, c0, c1):
+            return win_a[u][:].indirect(lists[name][:, c0 // 16 : c1 // 16])
+
+        def first_of(u, c0, c1):
+            base = plane("base")[:, : c1 - c0]
+            nc.vector.tensor_copy(base, looked_up(u, "n5", c0, c1))
+            return base
+
+        pieces = [(u, 0, N) for u in range(PACK)]
+        scores(0, -0.03125)
+        base = first_of(*pieces[0])
+        for u in range(1, PACK):
+            scores(u, -0.03125)
+        spare = plane("spare")
+        for k, (u, c0, c1) in enumerate(pieces[:-1]):
+            w = c1 - c0
+            d, e, v, g1, g2, g3, res = (plane(name)[:, :w] for name in ("d", "e", "v", "g1", "g2", "g3", "res"))
+            r = spare[:, :w]
+            nc.vector.tensor_tensor(d, looked_up(u, "n6", c0, c1), base, ALU.subtract)
+            nc.vector.tensor_tensor(e, looked_up(u, "n7", c0, c1), base, ALU.subtract)
+            nc.scalar.activation(r, d, ACT.Relu, scale=-1.0)
+            following = first_of(*pieces[k + 1])
+            nc.vector.scalar_tensor_tensor(v, d, 0.0, e, ALU.max, ALU.min)
+            level = turned_sum([base, v], w, k % 2)
+            spread = turned_sum([r, v], w, (k + 1) % 2)
+            nc.scalar.activation(g1, level, ACT.Copy, scale=-1.0)
+            nc.scalar.activation(g2, spread, ACT.Relu, scale=2.0)
+            nc.scalar.activation(g3, spread, ACT.Relu, scale=-1.0)
+            total = turned_sum([g1, g2, g3], w, 2)
+            nc.scalar.copy(res, total)
+            nc.sync.dma_start(out_rows[u][:, c0:c1], res)
+            spare, base = v, following
+
+        u = PACK - 1
+        d, least, e, low, lift, res = (plane(name) for name in ("d", "v", "e", "g2", "g3", "res"))
+        gap = spare
+        halves = [(0, N // 2), (N // 2, N)]
+        for c0, c1 in halves:
+            nc.vector.tensor_tensor(d[:, c0:c1], looked_up(u, "n6", c0, c1), base[:, c0:c1], ALU.subtract)
+            nc.scalar.activation(gap[:, c0:c1], d[:, c0:c1], ACT.Abs)
+        for c0, c1 in halves:
+            nc.vector.scalar_tensor_tensor(least[:, c0:c1], d[:, c0:c1], 0.0, base[:, c0:c1], ALU.min, ALU.add)
+        for c0, c1 in halves:
+            nc.vector.tensor_tensor(e[:, c0:c1], looked_up(u, "n7", c0, c1), least[:, c0:c1], ALU.subtract)
+        for c0, c1 in halves:
+            nc.vector.tensor_tensor(low[:, c0:c1], e[:, c0:c1], gap[:, c0:c1], ALU.min)
+        for c0, c1 in halves:
+            nc.vector.scalar_tensor_tensor(lift[:, c0:c1], e[:, c0:c1], -2.0, low[:, c0:c1], ALU.mult, ALU.max)
+        for c0, c1 in halves:
+            nc.vector.tensor_tensor(res[:, c0:c1], lift[:, c0:c1], least[:, c0:c1], ALU.subtract)
+            nc.sync.dma_start(out_rows[u][:, c0:c1], res[:, c0:c1])

@@ -18,6 +18,7 @@ PACK = 4
 N = 512
 T = 2048
 WIN = 2 * N
+HALF_BYTES = 4096
 
 FLOPS = 4 * 2 * 512 * 512 * 512
 
@@ -28,6 +29,7 @@ def tile_picked_twksoftbrmstop2_none_p_kernel(
     nc = tc.nc
     with ExitStack() as ctx:
         keep = ctx.enter_context(tc.tile_pool(name="keep", bufs=1))
+        stage = ctx.enter_context(tc.tile_pool(name="stage", bufs=1))
         ring = ctx.enter_context(tc.tile_pool(name="ring", bufs=4))
         psum = ctx.enter_context(tc.psum_pool(name="psum", bufs=1))
 
@@ -36,10 +38,10 @@ def tile_picked_twksoftbrmstop2_none_p_kernel(
             nc.sync.dma_start(tile[:], src)
             return tile
 
-        def load_weight(name, w):
+        def load_weight(name, w, place):
             halves = []
             for h in range(2):
-                raw = keep.tile([P, PACK, N // 2], F32, name="raw_%s_%d" % (name, h))
+                raw = stage.tile([P, PACK, N // 2], F32, name="raw_%s_%d" % (name, h), align_bytes=64, offset=(2 * place + h) * HALF_BYTES)
                 nc.sync.dma_start(raw[:], w.rearrange("(p j) c -> p j c", j=PACK)[:, :, h * (N // 2) : (h + 1) * (N // 2)])
                 halves.append(raw)
             return halves
@@ -53,36 +55,35 @@ def tile_picked_twksoftbrmstop2_none_p_kernel(
         lists["two"] = load_list("two", two)
         lists["three"] = load_list("three", three)
         lists["offs"] = load_list("offs", offs)
+        raw2 = load_weight("w2", w2, 0)
         xw = keep.tile([P, T], U32, name="xw", align_bytes=64)
         nc.sync.dma_start(xw[:].bitcast(I32), x_words[0].rearrange("p c r -> p (c r)").bitcast(I32))
-        raw2 = load_weight("w2", w2)
-        raw3 = load_weight("w3", w3)
+        raw3 = load_weight("w3", w3, 1)
         ga_t = keep.tile([P, PACK], F32, name="ga_t")
         gb_t = keep.tile([P, PACK], F32, name="gb_t")
         nc.sync.dma_start(ga_t[:], ga.rearrange("(p t) o -> p (t o)", t=PACK))
         lists["n2"] = load_list("n2", n2)
-        raw1 = load_weight("w1", w1)
+        raw1 = load_weight("w1", w1, 2)
         nc.sync.dma_start(gb_t[:], gb.rearrange("(p t) o -> p (t o)", t=PACK))
         for name, src in (("n3", n3), ("n4", n4), ("n1", n1), ("n5", n5), ("n6", n6), ("n7", n7)):
             lists[name] = load_list(name, src)
 
         win_a = [keep.tile([P, WIN], F32, name="win_a%d" % t) for t in range(PACK)]
         win_b = [keep.tile([P, WIN], F32, name="win_b%d" % t, align_bytes=64) for t in range(PACK)]
-        for win in win_a + win_b:
-            nc.vector.memset(win[:, N:], 0.0)
+        nc.vector.memset(win_a[0][:, N:], 0.0)
 
         def gather_scales(name):
             tile = keep.tile([P, N], U8, name="picked_scales_" + name, align_bytes=64)
             nc.vector.tensor_copy(tile[:], xs[:].indirect(lists[name][:]))
             return tile
 
-        def gather_words(name, tag=None):
-            tile = keep.tile([P, N], U32, name="picked_words_" + name, tag=tag or "picked_words_" + name, align_bytes=64)
+        def gather_words(name, offset):
+            tile = stage.tile([P, N], U32, name="picked_words_" + name, align_bytes=64, offset=offset)
             nc.vector.tensor_copy(tile[:], xw[:].indirect(lists[name][:]))
             return tile
 
-        def weave_weight(name, halves, copies):
-            woven = keep.tile([P, PACK * N], BF16, name="woven_" + name, align_bytes=64)
+        def weave_weight(halves, copies, name="woven_w"):
+            woven = keep.tile([P, PACK * N], BF16, name=name, align_bytes=64)
             dst = woven[:].rearrange("p (t m j) -> p m j t", t=PACK, j=PACK)
             for h, raw in enumerate(halves):
                 copies[h](dst[:, h * (P // 2) : (h + 1) * (P // 2)], raw[:].rearrange("p j (m t) -> p m j t", t=PACK))
@@ -115,16 +116,16 @@ def tile_picked_twksoftbrmstop2_none_p_kernel(
         make_identity(nc, ident[:])
 
         picked_scales = {name: gather_scales(name) for name in ("two", "three", "offs")}
-        woven2 = weave_weight("w2", raw2, (nc.scalar.copy, nc.scalar.copy))
-        woven3 = weave_weight("w3", raw3, (nc.scalar.copy, nc.scalar.copy))
-        q2 = quantize("w2", woven2, N)
+        q2 = quantize("w2", weave_weight(raw2, (nc.scalar.copy,nc.scalar.copy)), N)
+        x_two = (gather_words("two", HALF_BYTES), picked_scales["two"])
+        x_three = (gather_words("three", HALF_BYTES + HALF_BYTES // 2), picked_scales["three"])
+        woven3 = weave_weight(raw3, (nc.scalar.copy,nc.vector.tensor_copy))
+        x_offs = (gather_words("offs", 2 * HALF_BYTES), picked_scales["offs"])
         q3 = quantize("w3", woven3, N)
-        x_two = (gather_words("two"), picked_scales["two"])
-        x_three = (gather_words("three"), picked_scales["three"])
-        x_offs = (gather_words("offs", "woven_w2"), picked_scales["offs"])
 
-        tanh_d = keep.tile([P, PACK, N], F32, name="tanh_d")
-        prod = keep.tile([P, PACK, N], F32, name="prod")
+        tanh_last = keep.tile([P, N], F32, name="tanh_last")
+        tanh_d = [win[:, N:] for win in win_a[1:]] + [tanh_last[:]]
+        prod = [win_b[t - 1][:, N:] for t in range(PACK)]
         sq = keep.tile([P, PACK, N], F32, name="sq")
         den = keep.tile([P, PACK, N], F32, name="den")
         rs = keep.tile([P, PACK, N], F32, name="rs")
@@ -140,12 +141,13 @@ def tile_picked_twksoftbrmstop2_none_p_kernel(
         for t in range(PACK):
             acc = product(q2, t, x_two, t)
             nc.scalar.activation(win_a[t][:, :N], acc[:], ACT.Copy, scale=ga_t[:, t : t + 1])
-            nc.scalar.activation(tanh_d[:, t, :], acc[:], ACT.Tanh)
-            fused(prod[:, t, :], win_a[t], "n2", tanh_d[:, t, :], ALU.mult)
-            if t > 0:
-                square(t - 1)
-        square(PACK - 1)
-        woven1 = weave_weight("w1", raw1, (nc.scalar.copy, nc.scalar.copy))
+            nc.scalar.activation(tanh_d[t], acc[:], ACT.Tanh)
+            fused(prod[t], win_a[t], "n2", tanh_d[t], ALU.mult)
+            if t >= 2:
+                square(t - 2)
+        for t in range(PACK - 2, PACK):
+            square(t)
+        woven1 = weave_weight(raw1, (nc.scalar.copy, nc.scalar.copy))
         q1 = quantize("w1", woven1, N)
         for t in range(PACK):
             nc.scalar.activation(win_a[t][:, :N], acc_b[t][:], ACT.Copy, scale=gb_t[:, t : t + 1])
@@ -168,7 +170,7 @@ def tile_picked_twksoftbrmstop2_none_p_kernel(
             nc.vector.quantize_mx(out=codes_z2[:, cols].bitcast(FP8X4), scales=scales_z2[:, cols], in_=woven)
         qz2 = (codes_z2, scales_z2)
         for t in range(PACK):
-            fused(z[:, t * N : (t + 1) * N], win_b[t], "n1", prod[:, t, :], ALU.subtract)
+            fused(z[:, t * N : (t + 1) * N], win_b[t], "n1", prod[t], ALU.subtract)
 
         first = keep.tile([P, N], BF16, name="woven_z_first", align_bytes=64)
         rest = keep.tile([P, (PACK - 1) * N], BF16, name="woven_z_rest", align_bytes=64)
@@ -183,10 +185,22 @@ def tile_picked_twksoftbrmstop2_none_p_kernel(
         def scores(u, scale):
             src = first[:] if u == 0 else rest[:, (u - 1) * N : u * N]
             qz = quantize("zu%d" % u, src, P)
-            acc = product(qz, 0, qz2, PACK + u)
             if u == 0:
-                nc.vector.tensor_scalar(win_a[u][:, :N], acc[:], scale, None, ALU.mult)
+                for h in range(2):
+                    cols = slice(h * (N // 2), (h + 1) * (N // 2))
+                    acc = psum.tile([P, N // 2], F32, name="bank%d" % (3 + h))
+                    nc.tensor.matmul_mx(
+                        out=acc[:],
+                        lhsT=qz[0][:].bitcast(FP8X4),
+                        lhsT_scale=qz[1][:],
+                        rhs=qz2[0][:, cols].bitcast(FP8X4),
+                        rhs_scale=qz2[1][:, cols],
+                        start=True,
+                        stop=True,
+                    )
+                    nc.vector.tensor_scalar(win_a[u][:, cols], acc[:], scale, None, ALU.mult)
             else:
+                acc = product(qz, 0, qz2, PACK + u)
                 nc.scalar.activation(win_a[u][:, :N], acc[:], ACT.Copy, scale=scale)
 
         def turned_sum(terms, width, bank):
@@ -210,6 +224,7 @@ def tile_picked_twksoftbrmstop2_none_p_kernel(
         for u in range(1, PACK):
             scores(u, -0.03125)
         spare = plane("spare")
+        halves = [(0, N // 2), (N // 2, N)]
         for k, (u, c0, c1) in enumerate(pieces[:-1]):
             w = c1 - c0
             d, e, v, g1, g2, g3, res = (plane(name)[:, :w] for name in ("d", "e", "v", "g1", "g2", "g3", "res"))
@@ -219,23 +234,24 @@ def tile_picked_twksoftbrmstop2_none_p_kernel(
             nc.scalar.activation(r, d, ACT.Relu, scale=-1.0)
             following = first_of(*pieces[k + 1])
             nc.vector.scalar_tensor_tensor(v, d, 0.0, e, ALU.max, ALU.min)
-            level = turned_sum([base, v], w, k % 2)
-            spread = turned_sum([r, v], w, (k + 1) % 2)
-            nc.scalar.activation(g1, level, ACT.Copy, scale=-1.0)
+            spread = turned_sum([r, v], w, 0)
+            level = turned_sum([base, v], w, 1 + (k + 1) % 2)
             nc.scalar.activation(g2, spread, ACT.Relu, scale=2.0)
             nc.scalar.activation(g3, spread, ACT.Relu, scale=-1.0)
-            total = turned_sum([g1, g2, g3], w, 2)
+            if k == len(pieces) - 2:
+                last_d, gap = plane("d"), v
+                for h0, h1 in halves:
+                    nc.vector.tensor_tensor(last_d[:, h0:h1], looked_up(PACK - 1, "n6", h0, h1), following[:, h0:h1], ALU.subtract)
+                    nc.scalar.activation(gap[:, h0:h1], last_d[:, h0:h1], ACT.Abs)
+            nc.scalar.activation(g1, level, ACT.Copy, scale=-1.0)
+            total = turned_sum([g2, g3, g1], w, 1 + k % 2)
             nc.scalar.copy(res, total)
             nc.sync.dma_start(out_rows[u][:, c0:c1], res)
             spare, base = v, following
 
         u = PACK - 1
-        d, least, e, low, lift, res = (plane(name) for name in ("d", "v", "e", "g2", "g3", "res"))
-        gap = spare
-        halves = [(0, N // 2), (N // 2, N)]
-        for c0, c1 in halves:
-            nc.vector.tensor_tensor(d[:, c0:c1], looked_up(u, "n6", c0, c1), base[:, c0:c1], ALU.subtract)
-            nc.scalar.activation(gap[:, c0:c1], d[:, c0:c1], ACT.Abs)
+        least, e, low, lift, res = (plane(name) for name in ("v", "e", "g2", "g3", "res"))
+        d = last_d
         for c0, c1 in halves:
             nc.vector.scalar_tensor_tensor(least[:, c0:c1], d[:, c0:c1], 0.0, base[:, c0:c1], ALU.min, ALU.add)
         for c0, c1 in halves:

from contextlib import ExitStack

import concourse.mybir as mybir
from concourse.masks import make_identity

F32 = mybir.dt.float32
BF16 = mybir.dt.bfloat16
I32 = mybir.dt.int32
U32 = mybir.dt.uint32
U16 = mybir.dt.uint16
U8 = mybir.dt.uint8
FP8X4 = mybir.dt.float8_e4m3fn_x4
ALU = mybir.AluOpType
ACT = mybir.ActivationFunctionType

P = 128
PACK = 4
N = 512
T = 2048
WIN = 2 * N
HALF_BYTES = 4096

FLOPS = 4 * 2 * 512 * 512 * 512


def tile_picked_twksoftbrmstop2_none_p_kernel(
    tc, x_words, x_scales, w1, w2, w3, ga, gb, offs, two, n1, n2, three, n3, n4, n5, n6, n7, out
):
    nc = tc.nc
    with ExitStack() as ctx:
        keep = ctx.enter_context(tc.tile_pool(name="keep", bufs=1))
        stage = ctx.enter_context(tc.tile_pool(name="stage", bufs=1))
        ring = ctx.enter_context(tc.tile_pool(name="ring", bufs=4))
        psum = ctx.enter_context(tc.psum_pool(name="psum", bufs=1))

        def load_list(name, src):
            tile = keep.tile([P, N // 16], U16, name="list_" + name)
            nc.sync.dma_start(tile[:], src)
            return tile

        def load_weight(name, w, place):
            halves = []
            for h in range(2):
                raw = stage.tile([P, PACK, N // 2], F32, name="raw_%s_%d" % (name, h), align_bytes=64, offset=(2 * place + h) * HALF_BYTES)
                nc.sync.dma_start(raw[:], w.rearrange("(p j) c -> p j c", j=PACK)[:, :, h * (N // 2) : (h + 1) * (N // 2)])
                halves.append(raw)
            return halves

        xs = keep.tile([P, T], U8, name="xs", align_bytes=64)
        nc.vector.memset(xs[:].bitcast(I32), 0)
        for q in range(4):
            nc.scalar.dma_start(xs[32 * q : 32 * q + 4, :].bitcast(I32), x_scales[0, 4 * q : 4 * q + 4, :].bitcast(I32))

        lists = {}
        lists["two"] = load_list("two", two)
        lists["three"] = load_list("three", three)
        lists["offs"] = load_list("offs", offs)
        raw2 = load_weight("w2", w2, 0)
        xw = keep.tile([P, T], U32, name="xw", align_bytes=64)
        nc.sync.dma_start(xw[:].bitcast(I32), x_words[0].rearrange("p c r -> p (c r)").bitcast(I32))
        raw3 = load_weight("w3", w3, 1)
        ga_t = keep.tile([P, PACK], F32, name="ga_t")
        gb_t = keep.tile([P, PACK], F32, name="gb_t")
        nc.sync.dma_start(ga_t[:], ga.rearrange("(p t) o -> p (t o)", t=PACK))
        lists["n2"] = load_list("n2", n2)
        raw1 = load_weight("w1", w1, 2)
        nc.sync.dma_start(gb_t[:], gb.rearrange("(p t) o -> p (t o)", t=PACK))
        for name, src in (("n3", n3), ("n4", n4), ("n1", n1), ("n5", n5), ("n6", n6), ("n7", n7)):
            lists[name] = load_list(name, src)

        win_a = [keep.tile([P, WIN], F32, name="win_a%d" % t) for t in range(PACK)]
        win_b = [keep.tile([P, WIN], F32, name="win_b%d" % t, align_bytes=64) for t in range(PACK)]
        nc.vector.memset(win_a[0][:, N:], 0.0)

        def gather_scales(name):
            tile = keep.tile([P, N], U8, name="picked_scales_" + name, align_bytes=64)
            nc.vector.tensor_copy(tile[:], xs[:].indirect(lists[name][:]))
            return tile

        def gather_words(name, offset):
            tile = stage.tile([P, N], U32, name="picked_words_" + name, align_bytes=64, offset=offset)
            nc.vector.tensor_copy(tile[:], xw[:].indirect(lists[name][:]))
            return tile

        def weave_weight(halves, copies, name="woven_w"):
            woven = keep.tile([P, PACK * N], BF16, name=name, align_bytes=64)
            dst = woven[:].rearrange("p (t m j) -> p m j t", t=PACK, j=PACK)
            for h, raw in enumerate(halves):
                copies[h](dst[:, h * (P // 2) : (h + 1) * (P // 2)], raw[:].rearrange("p j (m t) -> p m j t", t=PACK))
            return woven

        def quantize(name, woven, width):
            codes = keep.tile([P, width], U32, name="codes_" + name, align_bytes=64)
            scales = keep.tile([P, width], U8, name="scales_" + name, align_bytes=64)
            nc.vector.quantize_mx(out=codes[:].bitcast(FP8X4), scales=scales[:], in_=woven[:])
            return codes, scales

        def product(stationary, t, moving, bank):
            acc = psum.tile([P, N], F32, name="bank%d" % bank)
            cols = slice(t * P, (t + 1) * P)
            nc.tensor.matmul_mx(
                out=acc[:],
                lhsT=stationary[0][:, cols].bitcast(FP8X4),
                lhsT_scale=stationary[1][:, cols],
                rhs=moving[0][:].bitcast(FP8X4),
                rhs_scale=moving[1][:],
                start=True,
                stop=True,
            )
            return acc

        def fused(dst, win, name, other, op):
            nc.vector.tensor_tensor(dst, win[:].indirect(lists[name][:]), other, op)

        ident = keep.tile([P, P], F32, name="ident")
        make_identity(nc, ident[:])

        picked_scales = {name: gather_scales(name) for name in ("two", "three", "offs")}
        q2 = quantize("w2", weave_weight(raw2, (nc.scalar.copy,nc.scalar.copy)), N)
        x_two = (gather_words("two", HALF_BYTES), picked_scales["two"])
        x_three = (gather_words("three", HALF_BYTES + HALF_BYTES // 2), picked_scales["three"])
        woven3 = weave_weight(raw3, (nc.scalar.copy,nc.vector.tensor_copy))
        x_offs = (gather_words("offs", 2 * HALF_BYTES), picked_scales["offs"])
        q3 = quantize("w3", woven3, N)

        tanh_last = keep.tile([P, N], F32, name="tanh_last")
        tanh_d = [win[:, N:] for win in win_a[1:]] + [tanh_last[:]]
        prod = [win_b[t - 1][:, N:] for t in range(PACK)]
        sq = keep.tile([P, PACK, N], F32, name="sq")
        den = keep.tile([P, PACK, N], F32, name="den")
        rs = keep.tile([P, PACK, N], F32, name="rs")
        z2 = keep.tile([P, PACK, N], F32, name="z2")
        z = keep.tile([P, PACK * N], F32, name="z", align_bytes=64)
        acc_b = []

        def square(t):
            acc_b.append(product(q3, t, x_three, PACK + t))
            nc.scalar.activation(win_b[t][:, :N], acc_b[t][:], ACT.Square)
            nc.sync.dma_start(sq[:, t, :], win_b[t][:, :N])

        for t in range(PACK):
            acc = product(q2, t, x_two, t)
            nc.scalar.activation(win_a[t][:, :N], acc[:], ACT.Copy, scale=ga_t[:, t : t + 1])
            nc.scalar.activation(tanh_d[t], acc[:], ACT.Tanh)
            fused(prod[t], win_a[t], "n2", tanh_d[t], ALU.mult)
            if t >= 2:
                square(t - 2)
        for t in range(PACK - 2, PACK):
            square(t)
        woven1 = weave_weight(raw1, (nc.scalar.copy, nc.scalar.copy))
        q1 = quantize("w1", woven1, N)
        for t in range(PACK):
            nc.scalar.activation(win_a[t][:, :N], acc_b[t][:], ACT.Copy, scale=gb_t[:, t : t + 1])
            fused(den[:, t, :], win_b[t], "n3", sq[:, t, :], ALU.add)
            nc.scalar.activation(rs[:, t, :], den[:, t, :], ACT.Abs_reciprocal_sqrt, bias=0.25)
        for t in range(PACK):
            fused(z2[:, t, :], win_a[t], "n4", rs[:, t, :], ALU.mult)
        for t in range(PACK):
            acc = product(q1, t, x_offs, t)
            nc.scalar.activation(win_b[t][:, :N], acc[:], ACT.Copy, scale=ga_t[:, t : t + 1])
        codes_z2 = keep.tile([P, N], U32, name="codes_z2", align_bytes=64)
        scales_z2 = keep.tile([P, N], U8, name="scales_z2", align_bytes=64)
        for h in range(2):
            cols = slice(h * (N // 2), (h + 1) * (N // 2))
            woven = z[:, (1 + h) * N : (2 + h) * N].bitcast(BF16)
            nc.scalar.copy(
                woven.rearrange("p (c i t) -> p c t i", i=4, t=PACK),
                z2[:, :, cols].rearrange("p t (c i) -> p c t i", i=4),
            )
            nc.vector.quantize_mx(out=codes_z2[:, cols].bitcast(FP8X4), scales=scales_z2[:, cols], in_=woven)
        qz2 = (codes_z2, scales_z2)
        for t in range(PACK):
            fused(z[:, t * N : (t + 1) * N], win_b[t], "n1", prod[t], ALU.subtract)

        first = keep.tile([P, N], BF16, name="woven_z_first", align_bytes=64)
        rest = keep.tile([P, (PACK - 1) * N], BF16, name="woven_z_rest", align_bytes=64)
        z_view = z[:].rearrange("p (t m u) -> p m t u", t=PACK, u=PACK)
        nc.vector.tensor_copy(first[:].rearrange("p (m t) -> p m t", t=PACK), z_view[:, :, :, 0])
        nc.scalar.copy(rest[:].rearrange("p (u m t) -> p m t u", u=PACK - 1, t=PACK), z_view[:, :, :, 1:])
        out_rows = out.rearrange("(p u) v -> u p v", u=PACK)

        def plane(name):
            return ring.tile([P, N], F32, name=name)

        def scores(u, scale):
            src = first[:] if u == 0 else rest[:, (u - 1) * N : u * N]
            qz = quantize("zu%d" % u, src, P)
            if u == 0:
                for h in range(2):
                    cols = slice(h * (N // 2), (h + 1) * (N // 2))
                    acc = psum.tile([P, N // 2], F32, name="bank%d" % (3 + h))
                    nc.tensor.matmul_mx(
                        out=acc[:],
                        lhsT=qz[0][:].bitcast(FP8X4),
                        lhsT_scale=qz[1][:],
                        rhs=qz2[0][:, cols].bitcast(FP8X4),
                        rhs_scale=qz2[1][:, cols],
                        start=True,
                        stop=True,
                    )
                    nc.vector.tensor_scalar(win_a[u][:, cols], acc[:], scale, None, ALU.mult)
            else:
                acc = product(qz, 0, qz2, PACK + u)
                nc.scalar.activation(win_a[u][:, :N], acc[:], ACT.Copy, scale=scale)

        def turned_sum(terms, width, bank):
            acc = psum.tile([P, N], F32, name="bank%d" % bank)
            steps = [(term, slice(b * P, (b + 1) * P)) for term in terms for b in range(width // P)]
            for k, (term, cols) in enumerate(steps):
                nc.tensor.matmul(acc[:, cols], term[:, cols], ident[:], start=k == 0, stop=k == len(steps) - 1, is_transpose=True)
            return acc[:, :width]

        def looked_up(u, name, c0, c1):
            return win_a[u][:].indirect(lists[name][:, c0 // 16 : c1 // 16])

        def first_of(u, c0, c1):
            base = plane("base")[:, : c1 - c0]
            nc.vector.tensor_copy(base, looked_up(u, "n5", c0, c1))
            return base

        pieces = [(u, 0, N) for u in range(PACK)]
        scores(0, -0.03125)
        base = first_of(*pieces[0])
        for u in range(1, PACK):
            scores(u, -0.03125)
        spare = plane("spare")
        halves = [(0, N // 2), (N // 2, N)]
        for k, (u, c0, c1) in enumerate(pieces[:-1]):
            w = c1 - c0
            d, e, v, g1, g2, g3, res = (plane(name)[:, :w] for name in ("d", "e", "v", "g1", "g2", "g3", "res"))
            r = spare[:, :w]
            nc.vector.tensor_tensor(d, looked_up(u, "n6", c0, c1), base, ALU.subtract)
            nc.vector.tensor_tensor(e, looked_up(u, "n7", c0, c1), base, ALU.subtract)
            nc.scalar.activation(r, d, ACT.Relu, scale=-1.0)
            following = first_of(*pieces[k + 1])
            nc.vector.scalar_tensor_tensor(v, d, 0.0, e, ALU.max, ALU.min)
            spread = turned_sum([r, v], w, 0)
            level = turned_sum([base, v], w, 1 + (k + 1) % 2)
            nc.scalar.activation(g2, spread, ACT.Relu, scale=2.0)
            nc.scalar.activation(g3, spread, ACT.Relu, scale=-1.0)
            if k == len(pieces) - 2:
                last_d, gap = plane("d"), v
                for h0, h1 in halves:
                    nc.vector.tensor_tensor(last_d[:, h0:h1], looked_up(PACK - 1, "n6", h0, h1), following[:, h0:h1], ALU.subtract)
                    nc.scalar.activation(gap[:, h0:h1], last_d[:, h0:h1], ACT.Abs)
            nc.scalar.activation(g1, level, ACT.Copy, scale=-1.0)
            total = turned_sum([g2, g3, g1], w, 1 + k % 2)
            nc.scalar.copy(res, total)
            nc.sync.dma_start(out_rows[u][:, c0:c1], res)
            spare, base = v, following

        u = PACK - 1
        least, e, low, lift, res = (plane(name) for name in ("v", "e", "g2", "g3", "res"))
        d = last_d
        for c0, c1 in halves:
            nc.vector.scalar_tensor_tensor(least[:, c0:c1], d[:, c0:c1], 0.0, base[:, c0:c1], ALU.min, ALU.add)
        for c0, c1 in halves:
            nc.vector.tensor_tensor(e[:, c0:c1], looked_up(u, "n7", c0, c1), least[:, c0:c1], ALU.subtract)
        for c0, c1 in halves:
            nc.vector.tensor_tensor(low[:, c0:c1], e[:, c0:c1], gap[:, c0:c1], ALU.min)
        for c0, c1 in halves:
            nc.vector.scalar_tensor_tensor(lift[:, c0:c1], e[:, c0:c1], -2.0, low[:, c0:c1], ALU.mult, ALU.max)
        for c0, c1 in halves:
            nc.vector.tensor_tensor(res[:, c0:c1], lift[:, c0:c1], least[:, c0:c1], ALU.subtract)
            nc.sync.dma_start(out_rows[u][:, c0:c1], res[:, c0:c1])
